import numpy as np
import ml_dtypes


def mxq(x, axis, fmt="e4m3"):
    dtype, down = {"e4m3": (ml_dtypes.float8_e4m3fn, 7), "e5m2": (ml_dtypes.float8_e5m2, 14)}[fmt]
    v = np.moveaxis(np.asarray(x, np.float32).astype(ml_dtypes.bfloat16).astype(np.float64), axis, -1)
    blocks = v.reshape(v.shape[:-1] + (-1, 32))
    amax = np.abs(blocks).max(-1, keepdims=True)
    byte = np.maximum(np.where(amax > 0, np.frexp(amax)[1] - 1 + 127, 0) - down, 1)
    scale = np.exp2(byte - 127.0)
    codes = (blocks / scale).astype(np.float32).astype(dtype).astype(np.float64)
    return np.moveaxis((codes * scale).reshape(v.shape), -1, axis)


WIDE = False


def mx_kscale(k):
    if not WIDE:
        return np.ones(k)
    levels = np.array([10, -10, 5, -5, 0])
    if k % 512:
        return np.exp2(np.random.permutation(np.resize(levels, k // 32))).repeat(32)
    a = np.empty((k // 512, 16))
    for p in range(k // 512):
        a[p, :8] = np.random.permutation(np.resize(levels, 8))
        for g in range(8):
            far = levels[np.abs(levels - a[p, g]) >= 10]
            a[p, g + 8] = far[np.random.randint(len(far))]
    return np.exp2(a.ravel()).repeat(32)


def f64(x):
    return np.asarray(x).astype(np.float64)


def striped(idx):
    return np.tile(idx.reshape(-1, 16).T, (8, 1)).astype(np.uint16)


def unstriped(offs):
    return offs[:16].T.reshape(-1).astype(np.int64)


E2M1 = np.array([0.0, 0.5, 1.0, 1.5, 2.0, 3.0, 4.0, 6.0, -0.0, -0.5, -1.0, -1.5, -2.0, -3.0, -4.0, -6.0])


def pack_weight(w, fmt):
    k, n = w.shape
    w = f64(np.asarray(w, np.float32).astype(ml_dtypes.bfloat16)).reshape(k // 32, 32, n)
    amax = np.abs(w).max(1)
    if fmt == "e4m3":
        byte = np.frexp(amax)[1] - 1 + 127 - 7
    else:
        mant, ex = np.frexp(amax / 6.0)
        byte = np.where(mant > 0.5, ex, ex - 1) + 127
    byte = np.clip(np.where(amax > 0, byte, 1), 1, 254)
    scaled = (w * np.exp2(127.0 - byte)[:, None, :]).reshape(k, n).astype(np.float32)
    by_word = np.ascontiguousarray(scaled.reshape(k // 512, 128, 4, n).transpose(0, 1, 3, 2))
    if fmt == "e4m3":
        words = by_word.astype(ml_dtypes.float8_e4m3fn).view(np.uint8)
    else:
        c = by_word.astype(ml_dtypes.float4_e2m1fn).view(np.uint8) & 0xF
        words = (c[..., 0::2] | (c[..., 1::2] << 4)).reshape(k // 512, 128, 2 * n)
    return np.ascontiguousarray(words), np.ascontiguousarray(byte.astype(np.uint8).reshape(k // 512, 16, n))


def unpack_weight(words, scales, fmt):
    g, _, n = scales.shape
    words = np.ascontiguousarray(words).reshape(g, 128, n, -1)
    if fmt == "e4m3":
        vals = words.view(ml_dtypes.float8_e4m3fn).astype(np.float64)
    else:
        nib = np.empty((g, 128, n, 4), np.uint8)
        nib[..., 0::2] = words & 0xF
        nib[..., 1::2] = words >> 4
        vals = E2M1[nib]
    vals = vals * np.repeat(np.exp2(scales.astype(np.float64) - 127.0), 8, axis=1)[..., None]
    return vals.transpose(0, 1, 3, 2).reshape(g * 512, n)


def d_relu(v):
    return (v > 0).astype(np.float64)


K, T, E, C, H, N = 128, 640, 2, 256, 1024, 1536


def by_expert(wq, xq):
    return np.concatenate([wq[e].T @ xq[:, e * C:(e + 1) * C] for e in range(E)], axis=1)


def setup_inputs():
    n = np.random.standard_normal
    s = mx_kscale(N)[:, None]
    u = mx_kscale(H)
    w2 = [pack_weight(m, "e2m1") for m in n((E, N, H)) / np.sqrt(N) / s[None] * u[None, None, :]]
    w1 = [pack_weight(m, "e2m1") for m in n((E, H, K)) / np.sqrt(H) / u[None, :, None]]
    return {
        "dyT": (n((N, T)) * s).astype(np.float32),
        "a": n((H, E * C)).astype(np.float32),
        "w2_words": np.stack([m[0] for m in w2]),
        "w2_scales": np.stack([m[1] for m in w2]),
        "w1_words": np.stack([m[0] for m in w1]),
        "w1_scales": np.stack([m[1] for m in w1]),
        "gate": np.tile(np.random.uniform(0.2, 1.0, E * C), (N, 1)).astype(np.float32),
        "offs": striped(np.random.permutation(T)[:E * C]),
    }


def reference(dyT, a, w2_words, w2_scales, w1_words, w1_scales, gate, offs):
    idx = unstriped(offs)
    w2 = np.stack([unpack_weight(w2_words[e], w2_scales[e], "e2m1") for e in range(E)])
    w1 = np.stack([unpack_weight(w1_words[e], w1_scales[e], "e2m1") for e in range(E)])
    gq = mxq(f64(gate) * f64(dyT)[:, idx], 0, "e4m3")
    dh = by_expert(w2, gq)
    da = dh * d_relu(f64(a))
    dx = by_expert(w1, mxq(da, 0, "e4m3"))
    out = np.zeros((K, T))
    out[:, idx] = dx
    return out

@@ -1,0 +1,234 @@
+from contextlib import ExitStack
+
+import concourse.mybir as mybir
+from concourse.masks import make_identity
+
+K, T, E, C, H, N = 128, 640, 2, 256, 1024, 1536
+S = E * C
+FLOPS = 2 * S * (N * H + H * K)
+BYTES = 4 * (N * T + H * S + S + K * T) + E * (N * H + H * K) * 17 // 32 + 2 * S
+
+F32 = mybir.dt.float32
+BF16 = mybir.dt.bfloat16
+U32 = mybir.dt.uint32
+I32 = mybir.dt.int32
+U16 = mybir.dt.uint16
+U8 = mybir.dt.uint8
+E4M3 = mybir.dt.float8_e4m3fn_x4
+E2M1 = mybir.dt.float4_e2m1fn_x4
+MULT = mybir.AluOpType.mult
+IS_GT = mybir.AluOpType.is_gt
+
+P = 128
+PASSES = N // 512
+HALVES = H // 512
+GROUPS = S // P
+
+
+def tile_moe_bdx_mlp_relu_kernel(
+    tc, dyT, a, w2_words, w2_scales, w1_words, w1_scales, gate, offs, out
+):
+    nc = tc.nc
+    with ExitStack() as ctx:
+        held = ctx.enter_context(tc.tile_pool(name="held", bufs=1))
+        work = ctx.enter_context(tc.tile_pool(name="work", bufs=3))
+        dh_pool = ctx.enter_context(tc.psum_pool(name="dh_pool", bufs=5))
+        xt_pool = ctx.enter_context(tc.psum_pool(name="xt_pool", bufs=2))
+        o_pool = ctx.enter_context(tc.psum_pool(name="o_pool", bufs=1))
+
+        offsets = held.tile([P, S // 16], U16, name="offsets")
+        nc.sync.dma_start(offsets[:], offs)
+
+        gate_sb = [held.tile([P, C], F32, name=f"gate_sb{i}") for i in range(3)]
+        w2_planes = held.tile([P, E * PASSES, H], U8, name="w2_planes", align_bytes=64)
+        w1_planes = held.tile([P, E * HALVES, K], U8, name="w1_planes", align_bytes=64)
+        window = held.tile([P, T], F32, name="window")
+        identity = held.tile([P, P], F32, name="identity")
+        nc.gpsimd.memset(w2_planes[:].rearrange("p n c -> p (n c)").bitcast(I32), 0)
+        nc.gpsimd.memset(w1_planes[:].rearrange("p n c -> p (n c)").bitcast(I32), 0)
+        make_identity(nc, identity[:])
+        nc.gpsimd.memset(window[:], 0.0)
+
+        dy_view = dyT.rearrange("(s p d) t -> s d p t", p=P, d=4)
+        dy = [[held.tile([P, T], F32, name=f"dy{s}_{d}") for d in range(4)] for s in range(PASSES)]
+        w2_sb = [held.tile([P, PASSES, 2 * H], U8, name=f"w2_sb{e}", align_bytes=64) for e in range(E)]
+        w1_sb = held.tile([P, E * HALVES, 2 * K], U8, name="w1_sb", align_bytes=64)
+        a_sb = [held.tile([P, HALVES, 4, C], F32, name=f"a_sb{e}") for e in range(E)]
+        a_view = a.rearrange("(h p d) c -> h p d c", p=P, d=4)
+
+        def load_dy(s):
+            for d in range(4):
+                nc.sync.dma_start(dy[s][d][:], dy_view[s, d])
+
+        def load_w2(e):
+            nc.sync.dma_start(w2_sb[e][:].bitcast(I32), w2_words[e].rearrange("s p c -> p s c").bitcast(I32))
+
+        def load_a(e):
+            for h in range(HALVES):
+                nc.sync.dma_start(a_sb[e][:, h, :, :], a_view[h, :, :, e * C : (e + 1) * C])
+
+        def load_scales(planes, scales):
+            by_pass = scales.rearrange("e s f c -> (e s) f c")
+            for quad in range(4):
+                nc.sync.dma_start(
+                    planes[32 * quad : 32 * quad + 4, :, :].bitcast(I32),
+                    by_pass[:, 4 * quad : 4 * quad + 4, :].rearrange("n r c -> r n c").bitcast(I32),
+                )
+
+        nc.sync.dma_start(gate_sb[0][:], gate[0:P, 0:C])
+        load_dy(0)
+        load_dy(1)
+        nc.sync.dma_start(gate_sb[1][:], gate[0:P, C:S])
+        load_scales(w2_planes, w2_scales)
+        load_w2(0)
+        load_dy(2)
+        nc.sync.dma_start(gate_sb[2][:], gate[P : 2 * P, C:S])
+        load_a(0)
+        load_w2(1)
+        load_scales(w1_planes, w1_scales)
+        nc.sync.dma_start(w1_sb[:].bitcast(I32), w1_words.rearrange("e s p c -> p (e s) c").bitcast(I32))
+        load_a(1)
+
+        g_codes, g_scales, g_wide = {}, {}, {}
+
+        def gather(s, lo, n):
+            gate_of = gate_sb[0 if lo == 0 else 1 if s == 0 else 2]
+            g = work.tile([P, 4, n], F32, name="g")
+            for d in range(4):
+                nc.vector.tensor_tensor(
+                    g[:, d, :],
+                    dy[s][d][:].indirect(offsets[:, lo // 16 : (lo + n) // 16]),
+                    gate_of[:],
+                    MULT,
+                )
+            wide = work.tile([P, n, 4], BF16, name="wide", align_bytes=64)
+            nc.scalar.copy(wide[:], g[:].rearrange("p d c -> p c d"))
+            g_wide[s, lo] = wide
+
+        def quantize_g(s, lo, n):
+            codes = held.tile([P, n], U32, name=f"g_codes{s}_{lo}", align_bytes=64)
+            scales = held.tile([P, n], U8, name=f"g_scales{s}_{lo}", align_bytes=64)
+            nc.vector.quantize_mx(
+                out=codes[:].bitcast(E4M3), scales=scales[:], in_=g_wide[s, lo][:].rearrange("p c d -> p (c d)")
+            )
+            for q in range(lo // P, (lo + n) // P):
+                cols = slice(q * P - lo, q * P - lo + P)
+                g_codes[s, q] = codes[:, cols]
+                g_scales[s, q] = scales[:, cols]
+
+        dh, xts, live, das, codes2 = {}, {}, {}, {}, {}
+
+        def multiply_w2(q, passes):
+            e = q * P // C
+            for h in range(HALVES):
+                if 0 in passes:
+                    dh[q, h] = dh_pool.tile([P, 512], F32, name="dh")
+                for s in passes:
+                    nc.tensor.matmul_mx(
+                        out=dh[q, h][:],
+                        lhsT=g_codes[s, q].bitcast(E4M3),
+                        lhsT_scale=g_scales[s, q],
+                        rhs=w2_sb[e][:, s, 1024 * h : 1024 * (h + 1)].bitcast(E2M1),
+                        rhs_scale=w2_planes[:, e * PASSES + s, 512 * h : 512 * (h + 1)],
+                        start=(s == 0),
+                        stop=(s == PASSES - 1),
+                    )
+
+        def turn(q):
+            xts[q] = xt_pool.tile([P, HALVES, P, 2], F32, name="xt")
+            for h in range(HALVES):
+                dhb = work.tile([P, 2, 256], BF16, name="dhb")
+                nc.scalar.copy(
+                    dhb[:].rearrange("c u (p b) -> c u p b", b=2),
+                    dh[q, h][:].rearrange("c (p u b) -> c u p b", u=2, b=2),
+                )
+                for u in range(2):
+                    nc.tensor.transpose(xts[q][:, h, :, u], dhb[:, u, :].bitcast(F32), identity[:])
+
+        def make_mask(e):
+            live[e] = held.tile([P, HALVES, C, 4], BF16, name=f"mask{e}", tag=f"dy2_{3 - e}")
+            for h in range(HALVES):
+                nc.vector.tensor_scalar(
+                    live[e][:, h, :, :], a_sb[e][:, h, :, :].rearrange("p d c -> p c d"), 0.0, None, IS_GT
+                )
+
+        def mask(q):
+            e, lo = q * P // C, q * P % C
+            das[q] = work.tile([P, HALVES, P, 4], BF16, name="da", align_bytes=64)
+            nc.vector.tensor_tensor(
+                das[q][:].rearrange("p h c d -> p h (c d)"),
+                xts[q][:].rearrange("p h c u -> p h (c u)").bitcast(BF16),
+                live[e][:, :, lo : lo + P, :].rearrange("p h c d -> p h (c d)"),
+                MULT,
+            )
+
+        def quantize_da(q):
+            codes = work.tile([P, HALVES * P], U32, name="da_codes", align_bytes=64)
+            scales = work.tile([P, HALVES * P], U8, name="da_scales", align_bytes=64)
+            nc.vector.quantize_mx(
+                out=codes[:].bitcast(E4M3), scales=scales[:], in_=das[q][:].rearrange("p h c d -> p (h c d)")
+            )
+            codes2[q] = codes, scales
+
+        def multiply_w1(q, dx_sb):
+            e = q * P // C
+            codes, scales = codes2[q]
+            dx = o_pool.tile([P, P], F32, name="dx")
+            for h in range(HALVES):
+                cols = slice(h * P, (h + 1) * P)
+                nc.tensor.matmul_mx(
+                    out=dx[:],
+                    lhsT=w1_sb[:, e * HALVES + h, :].bitcast(E2M1),
+                    lhsT_scale=w1_planes[:, e * HALVES + h, :],
+                    rhs=codes[:, cols].bitcast(E4M3),
+                    rhs_scale=scales[:, cols],
+                    start=(h == 0),
+                    stop=(h == HALVES - 1),
+                )
+            nc.scalar.copy(dx_sb, dx[:])
+
+        def scatter(lo, n, dx_sb):
+            nc.vector.tensor_copy(window[:].indirect(offsets[:, lo // 16 : (lo + n) // 16]), dx_sb)
+
+        every = range(PASSES)
+        gather(0, 0, C)
+        gather(1, 0, C)
+        quantize_g(0, 0, C)
+        gather(2, 0, C)
+        quantize_g(1, 0, C)
+        quantize_g(2, 0, C)
+        multiply_w2(0, every)
+        turn(0)
+        multiply_w2(1, every)
+        turn(1)
+        gather(0, C, C)
+        gather(1, C, C)
+        quantize_g(0, C, C)
+        gather(2, C, C)
+        quantize_g(1, C, C)
+        quantize_g(2, C, C)
+        make_mask(0)
+        mask(0)
+        mask(1)
+        dx01 = held.tile([P, C], F32, name="dx01")
+        quantize_da(0)
+        multiply_w1(0, dx01[:, 0:P])
+        quantize_da(1)
+        multiply_w1(1, dx01[:, P:C])
+        multiply_w2(2, every)
+        turn(2)
+        multiply_w2(3, every)
+        turn(3)
+        scatter(0, C, dx01[:])
+        make_mask(1)
+        mask(2)
+        quantize_da(2)
+        dx2 = held.tile([P, P], F32, name="dx2")
+        multiply_w1(2, dx2[:])
+        mask(3)
+        quantize_da(3)
+        dx3 = held.tile([P, P], F32, name="dx3")
+        multiply_w1(3, dx3[:])
+        scatter(C, P, dx2[:])
+        scatter(C + P, P, dx3[:])
+        nc.sync.dma_start(out, window[:])

@@ -53,7 +53,7 @@ def tile_moe_bdx_mlp_relu_kernel(
         dy = [[held.tile([P, T], F32, name=f"dy{s}_{d}") for d in range(4)] for s in range(PASSES)]
         w2_sb = [held.tile([P, PASSES, 2 * H], U8, name=f"w2_sb{e}", align_bytes=64) for e in range(E)]
         w1_sb = held.tile([P, E * HALVES, 2 * K], U8, name="w1_sb", align_bytes=64)
-        a_sb = [held.tile([P, HALVES, 4, C], F32, name=f"a_sb{e}") for e in range(E)]
+        a_sb = [held.tile([P, 4, S], F32, name=f"a_sb{h}") for h in range(HALVES)]
         a_view = a.rearrange("(h p d) c -> h p d c", p=P, d=4)
 
         def load_dy(s):
@@ -62,10 +62,6 @@ def tile_moe_bdx_mlp_relu_kernel(
 
         def load_w2(e):
             nc.sync.dma_start(w2_sb[e][:].bitcast(I32), w2_words[e].rearrange("s p c -> p s c").bitcast(I32))
-
-        def load_a(e):
-            for h in range(HALVES):
-                nc.sync.dma_start(a_sb[e][:, h, :, :], a_view[h, :, :, e * C : (e + 1) * C])
 
         def load_scales(planes, scales):
             by_pass = scales.rearrange("e s f c -> (e s) f c")
@@ -79,15 +75,15 @@ def tile_moe_bdx_mlp_relu_kernel(
         load_dy(0)
         load_dy(1)
         nc.sync.dma_start(gate_sb[1][:], gate[0:P, C:S])
-        load_scales(w2_planes, w2_scales)
-        load_w2(0)
         load_dy(2)
         nc.sync.dma_start(gate_sb[2][:], gate[P : 2 * P, C:S])
-        load_a(0)
-        load_w2(1)
+        load_w2(0)
+        load_scales(w2_planes, w2_scales)
         load_scales(w1_planes, w1_scales)
+        load_w2(1)
+        for h in range(HALVES):
+            nc.sync.dma_start(a_sb[h][:], a_view[h])
         nc.sync.dma_start(w1_sb[:].bitcast(I32), w1_words.rearrange("e s p c -> p (e s) c").bitcast(I32))
-        load_a(1)
 
         g_codes, g_scales, g_wide = {}, {}, {}
 
@@ -102,7 +98,9 @@ def tile_moe_bdx_mlp_relu_kernel(
                     MULT,
                 )
             wide = work.tile([P, n, 4], BF16, name="wide", align_bytes=64)
-            nc.scalar.copy(wide[:], g[:].rearrange("p d c -> p c d"))
+            nc.scalar.copy(
+                wide[:].rearrange("p (c i) d -> p c d i", i=4), g[:].rearrange("p d (c i) -> p c d i", i=4)
+            )
             g_wide[s, lo] = wide
 
         def quantize_g(s, lo, n):
@@ -149,7 +147,7 @@ def tile_moe_bdx_mlp_relu_kernel(
             live[e] = held.tile([P, HALVES, C, 4], BF16, name=f"mask{e}", tag=f"dy2_{3 - e}")
             for h in range(HALVES):
                 nc.vector.tensor_scalar(
-                    live[e][:, h, :, :], a_sb[e][:, h, :, :].rearrange("p d c -> p c d"), 0.0, None, IS_GT
+                    live[e][:, h, :, :], a_sb[h][:, :, e * C : (e + 1) * C].rearrange("p d c -> p c d"), 0.0, None, IS_GT
                 )
 
         def mask(q):

@@ -53,7 +53,7 @@ def tile_moe_bdx_mlp_relu_kernel(
         dy = [[held.tile([P, T], F32, name=f"dy{s}_{d}") for d in range(4)] for s in range(PASSES)]
         w2_sb = [held.tile([P, PASSES, 2 * H], U8, name=f"w2_sb{e}", align_bytes=64) for e in range(E)]
         w1_sb = held.tile([P, E * HALVES, 2 * K], U8, name="w1_sb", align_bytes=64)
-        a_sb = [held.tile([P, 4, S], F32, name=f"a_sb{h}") for h in range(HALVES)]
+        a_sb = [held.tile([P, HALVES, 4, C], F32, name=f"a_sb{e}") for e in range(E)]
         a_view = a.rearrange("(h p d) c -> h p d c", p=P, d=4)
 
         def load_dy(s):
@@ -62,6 +62,10 @@ def tile_moe_bdx_mlp_relu_kernel(
 
         def load_w2(e):
             nc.sync.dma_start(w2_sb[e][:].bitcast(I32), w2_words[e].rearrange("s p c -> p s c").bitcast(I32))
+
+        def load_a(e):
+            for h in range(HALVES):
+                nc.sync.dma_start(a_sb[e][:, h, :, :], a_view[h, :, :, e * C : (e + 1) * C])
 
         def load_scales(planes, scales):
             by_pass = scales.rearrange("e s f c -> (e s) f c")
@@ -81,8 +85,8 @@ def tile_moe_bdx_mlp_relu_kernel(
         load_scales(w2_planes, w2_scales)
         load_scales(w1_planes, w1_scales)
         load_w2(1)
-        for h in range(HALVES):
-            nc.sync.dma_start(a_sb[h][:], a_view[h])
+        load_a(0)
+        load_a(1)
         nc.sync.dma_start(w1_sb[:].bitcast(I32), w1_words.rearrange("e s p c -> p (e s) c").bitcast(I32))
 
         g_codes, g_scales, g_wide = {}, {}, {}
@@ -147,7 +151,7 @@ def tile_moe_bdx_mlp_relu_kernel(
             live[e] = held.tile([P, HALVES, C, 4], BF16, name=f"mask{e}", tag=f"dy2_{3 - e}")
             for h in range(HALVES):
                 nc.vector.tensor_scalar(
-                    live[e][:, h, :, :], a_sb[h][:, :, e * C : (e + 1) * C].rearrange("p d c -> p c d"), 0.0, None, IS_GT
+                    live[e][:, h, :, :], a_sb[e][:, h, :, :].rearrange("p d c -> p c d"), 0.0, None, IS_GT
                 )
 
         def mask(q):
@@ -194,36 +198,38 @@ def tile_moe_bdx_mlp_relu_kernel(
         quantize_g(0, 0, C)
         gather(2, 0, C)
         quantize_g(1, 0, C)
+        gather(0, C, C)
         quantize_g(2, 0, C)
         multiply_w2(0, every)
-        turn(0)
         multiply_w2(1, every)
-        turn(1)
-        gather(0, C, C)
         gather(1, C, C)
-        quantize_g(0, C, C)
+        turn(0)
         gather(2, C, C)
+        turn(1)
+        quantize_g(0, C, C)
         quantize_g(1, C, C)
-        quantize_g(2, C, C)
+        multiply_w2(2, (0, 1))
+        multiply_w2(3, (0, 1))
         make_mask(0)
         mask(0)
+        quantize_g(2, C, C)
+        multiply_w2(2, (2,))
+        multiply_w2(3, (2,))
         mask(1)
         dx01 = held.tile([P, C], F32, name="dx01")
         quantize_da(0)
         multiply_w1(0, dx01[:, 0:P])
         quantize_da(1)
         multiply_w1(1, dx01[:, P:C])
-        multiply_w2(2, every)
         turn(2)
-        multiply_w2(3, every)
+        make_mask(1)
         turn(3)
         scatter(0, C, dx01[:])
-        make_mask(1)
         mask(2)
+        mask(3)
         quantize_da(2)
         dx2 = held.tile([P, P], F32, name="dx2")
         multiply_w1(2, dx2[:])
-        mask(3)
         quantize_da(3)
         dx3 = held.tile([P, P], F32, name="dx3")
         multiply_w1(3, dx3[:])

from contextlib import ExitStack

import concourse.mybir as mybir
from concourse.masks import make_identity

K, T, E, C, H, N = 128, 640, 2, 256, 1024, 1536
S = E * C
FLOPS = 2 * S * (N * H + H * K)
BYTES = 4 * (N * T + H * S + S + K * T) + E * (N * H + H * K) * 17 // 32 + 2 * S

F32 = mybir.dt.float32
BF16 = mybir.dt.bfloat16
U32 = mybir.dt.uint32
I32 = mybir.dt.int32
U16 = mybir.dt.uint16
U8 = mybir.dt.uint8
E4M3 = mybir.dt.float8_e4m3fn_x4
E2M1 = mybir.dt.float4_e2m1fn_x4
MULT = mybir.AluOpType.mult
IS_GT = mybir.AluOpType.is_gt

P = 128
PASSES = N // 512
HALVES = H // 512
GROUPS = S // P


def tile_moe_bdx_mlp_relu_kernel(
    tc, dyT, a, w2_words, w2_scales, w1_words, w1_scales, gate, offs, out
):
    nc = tc.nc
    with ExitStack() as ctx:
        held = ctx.enter_context(tc.tile_pool(name="held", bufs=1))
        work = ctx.enter_context(tc.tile_pool(name="work", bufs=3))
        dh_pool = ctx.enter_context(tc.psum_pool(name="dh_pool", bufs=5))
        xt_pool = ctx.enter_context(tc.psum_pool(name="xt_pool", bufs=2))
        o_pool = ctx.enter_context(tc.psum_pool(name="o_pool", bufs=1))

        offsets = held.tile([P, S // 16], U16, name="offsets")
        nc.sync.dma_start(offsets[:], offs)

        gate_sb = [held.tile([P, C], F32, name=f"gate_sb{i}") for i in range(3)]
        w2_planes = held.tile([P, E * PASSES, H], U8, name="w2_planes", align_bytes=64)
        w1_planes = held.tile([P, E * HALVES, K], U8, name="w1_planes", align_bytes=64)
        window = held.tile([P, T], F32, name="window")
        identity = held.tile([P, P], F32, name="identity")
        nc.gpsimd.memset(w2_planes[:].rearrange("p n c -> p (n c)").bitcast(I32), 0)
        nc.gpsimd.memset(w1_planes[:].rearrange("p n c -> p (n c)").bitcast(I32), 0)
        make_identity(nc, identity[:])
        nc.gpsimd.memset(window[:], 0.0)

        dy_view = dyT.rearrange("(s p d) t -> s d p t", p=P, d=4)
        dy = [[held.tile([P, T], F32, name=f"dy{s}_{d}") for d in range(4)] for s in range(PASSES)]
        w2_sb = [held.tile([P, PASSES, 2 * H], U8, name=f"w2_sb{e}", align_bytes=64) for e in range(E)]
        w1_sb = held.tile([P, E * HALVES, 2 * K], U8, name="w1_sb", align_bytes=64)
        a_sb = [held.tile([P, HALVES, 4, C], F32, name=f"a_sb{e}") for e in range(E)]
        a_view = a.rearrange("(h p d) c -> h p d c", p=P, d=4)

        def load_dy(s):
            for d in range(4):
                nc.sync.dma_start(dy[s][d][:], dy_view[s, d])

        def load_w2(e):
            nc.sync.dma_start(w2_sb[e][:].bitcast(I32), w2_words[e].rearrange("s p c -> p s c").bitcast(I32))

        def load_a(e):
            for h in range(HALVES):
                nc.sync.dma_start(a_sb[e][:, h, :, :], a_view[h, :, :, e * C : (e + 1) * C])

        def load_scales(planes, scales):
            by_pass = scales.rearrange("e s f c -> (e s) f c")
            for quad in range(4):
                nc.sync.dma_start(
                    planes[32 * quad : 32 * quad + 4, :, :].bitcast(I32),
                    by_pass[:, 4 * quad : 4 * quad + 4, :].rearrange("n r c -> r n c").bitcast(I32),
                )

        nc.sync.dma_start(gate_sb[0][:], gate[0:P, 0:C])
        load_dy(0)
        load_dy(1)
        nc.sync.dma_start(gate_sb[1][:], gate[0:P, C:S])
        load_dy(2)
        nc.sync.dma_start(gate_sb[2][:], gate[P : 2 * P, C:S])
        load_w2(0)
        load_scales(w2_planes, w2_scales)
        load_scales(w1_planes, w1_scales)
        load_w2(1)
        load_a(0)
        load_a(1)
        nc.sync.dma_start(w1_sb[:].bitcast(I32), w1_words.rearrange("e s p c -> p (e s) c").bitcast(I32))

        g_codes, g_scales, g_wide = {}, {}, {}

        def gather(s, lo, n):
            gate_of = gate_sb[0 if lo == 0 else 1 if s == 0 else 2]
            g = work.tile([P, 4, n], F32, name="g")
            for d in range(4):
                nc.vector.tensor_tensor(
                    g[:, d, :],
                    dy[s][d][:].indirect(offsets[:, lo // 16 : (lo + n) // 16]),
                    gate_of[:],
                    MULT,
                )
            wide = work.tile([P, n, 4], BF16, name="wide", align_bytes=64)
            nc.scalar.copy(
                wide[:].rearrange("p (c i) d -> p c d i", i=4), g[:].rearrange("p d (c i) -> p c d i", i=4)
            )
            g_wide[s, lo] = wide

        def quantize_g(s, lo, n):
            codes = held.tile([P, n], U32, name=f"g_codes{s}_{lo}", align_bytes=64)
            scales = held.tile([P, n], U8, name=f"g_scales{s}_{lo}", align_bytes=64)
            nc.vector.quantize_mx(
                out=codes[:].bitcast(E4M3), scales=scales[:], in_=g_wide[s, lo][:].rearrange("p c d -> p (c d)")
            )
            for q in range(lo // P, (lo + n) // P):
                cols = slice(q * P - lo, q * P - lo + P)
                g_codes[s, q] = codes[:, cols]
                g_scales[s, q] = scales[:, cols]

        dh, xts, live, das, codes2 = {}, {}, {}, {}, {}

        def multiply_w2(q, passes):
            e = q * P // C
            for h in range(HALVES):
                if 0 in passes:
                    dh[q, h] = dh_pool.tile([P, 512], F32, name="dh")
                for s in passes:
                    nc.tensor.matmul_mx(
                        out=dh[q, h][:],
                        lhsT=g_codes[s, q].bitcast(E4M3),
                        lhsT_scale=g_scales[s, q],
                        rhs=w2_sb[e][:, s, 1024 * h : 1024 * (h + 1)].bitcast(E2M1),
                        rhs_scale=w2_planes[:, e * PASSES + s, 512 * h : 512 * (h + 1)],
                        start=(s == 0),
                        stop=(s == PASSES - 1),
                    )

        def turn(q):
            xts[q] = xt_pool.tile([P, HALVES, P, 2], F32, name="xt")
            for h in range(HALVES):
                dhb = work.tile([P, 2, 256], BF16, name="dhb")
                nc.scalar.copy(
                    dhb[:].rearrange("c u (p b) -> c u p b", b=2),
                    dh[q, h][:].rearrange("c (p u b) -> c u p b", u=2, b=2),
                )
                for u in range(2):
                    nc.tensor.transpose(xts[q][:, h, :, u], dhb[:, u, :].bitcast(F32), identity[:])

        def make_mask(e):
            live[e] = held.tile([P, HALVES, C, 4], BF16, name=f"mask{e}", tag=f"dy2_{3 - e}")
            for h in range(HALVES):
                nc.vector.tensor_scalar(
                    live[e][:, h, :, :], a_sb[e][:, h, :, :].rearrange("p d c -> p c d"), 0.0, None, IS_GT
                )

        def mask(q):
            e, lo = q * P // C, q * P % C
            das[q] = work.tile([P, HALVES, P, 4], BF16, name="da", align_bytes=64)
            nc.vector.tensor_tensor(
                das[q][:].rearrange("p h c d -> p h (c d)"),
                xts[q][:].rearrange("p h c u -> p h (c u)").bitcast(BF16),
                live[e][:, :, lo : lo + P, :].rearrange("p h c d -> p h (c d)"),
                MULT,
            )

        def quantize_da(q):
            codes = work.tile([P, HALVES * P], U32, name="da_codes", align_bytes=64)
            scales = work.tile([P, HALVES * P], U8, name="da_scales", align_bytes=64)
            nc.vector.quantize_mx(
                out=codes[:].bitcast(E4M3), scales=scales[:], in_=das[q][:].rearrange("p h c d -> p (h c d)")
            )
            codes2[q] = codes, scales

        def multiply_w1(q, dx_sb):
            e = q * P // C
            codes, scales = codes2[q]
            dx = o_pool.tile([P, P], F32, name="dx")
            for h in range(HALVES):
                cols = slice(h * P, (h + 1) * P)
                nc.tensor.matmul_mx(
                    out=dx[:],
                    lhsT=w1_sb[:, e * HALVES + h, :].bitcast(E2M1),
                    lhsT_scale=w1_planes[:, e * HALVES + h, :],
                    rhs=codes[:, cols].bitcast(E4M3),
                    rhs_scale=scales[:, cols],
                    start=(h == 0),
                    stop=(h == HALVES - 1),
                )
            nc.scalar.copy(dx_sb, dx[:])

        def scatter(lo, n, dx_sb):
            nc.vector.tensor_copy(window[:].indirect(offsets[:, lo // 16 : (lo + n) // 16]), dx_sb)

        every = range(PASSES)
        gather(0, 0, C)
        gather(1, 0, C)
        quantize_g(0, 0, C)
        gather(2, 0, C)
        quantize_g(1, 0, C)
        gather(0, C, C)
        quantize_g(2, 0, C)
        multiply_w2(0, every)
        multiply_w2(1, every)
        gather(1, C, C)
        turn(0)
        gather(2, C, C)
        turn(1)
        quantize_g(0, C, C)
        quantize_g(1, C, C)
        multiply_w2(2, (0, 1))
        multiply_w2(3, (0, 1))
        make_mask(0)
        mask(0)
        quantize_g(2, C, C)
        multiply_w2(2, (2,))
        multiply_w2(3, (2,))
        mask(1)
        dx01 = held.tile([P, C], F32, name="dx01")
        quantize_da(0)
        multiply_w1(0, dx01[:, 0:P])
        quantize_da(1)
        multiply_w1(1, dx01[:, P:C])
        turn(2)
        make_mask(1)
        turn(3)
        scatter(0, C, dx01[:])
        mask(2)
        mask(3)
        quantize_da(2)
        dx2 = held.tile([P, P], F32, name="dx2")
        multiply_w1(2, dx2[:])
        quantize_da(3)
        dx3 = held.tile([P, P], F32, name="dx3")
        multiply_w1(3, dx3[:])
        scatter(C, P, dx2[:])
        scatter(C + P, P, dx3[:])
        nc.sync.dma_start(out, window[:])
